import numpy as np
import ml_dtypes


def mxq(x, axis, fmt="e4m3"):
    dtype, down = {"e4m3": (ml_dtypes.float8_e4m3fn, 7), "e5m2": (ml_dtypes.float8_e5m2, 14)}[fmt]
    v = np.moveaxis(np.asarray(x, np.float32).astype(ml_dtypes.bfloat16).astype(np.float64), axis, -1)
    blocks = v.reshape(v.shape[:-1] + (-1, 32))
    amax = np.abs(blocks).max(-1, keepdims=True)
    byte = np.maximum(np.where(amax > 0, np.frexp(amax)[1] - 1 + 127, 0) - down, 1)
    scale = np.exp2(byte - 127.0)
    codes = (blocks / scale).astype(np.float32).astype(dtype).astype(np.float64)
    return np.moveaxis((codes * scale).reshape(v.shape), -1, axis)


WIDE = False


def mx_kscale(k):
    if not WIDE:
        return np.ones(k)
    levels = np.array([10, -10, 5, -5, 0])
    if k % 512:
        return np.exp2(np.random.permutation(np.resize(levels, k // 32))).repeat(32)
    a = np.empty((k // 512, 16))
    for p in range(k // 512):
        a[p, :8] = np.random.permutation(np.resize(levels, 8))
        for g in range(8):
            far = levels[np.abs(levels - a[p, g]) >= 10]
            a[p, g + 8] = far[np.random.randint(len(far))]
    return np.exp2(a.ravel()).repeat(32)


def f64(x):
    return np.asarray(x).astype(np.float64)


def striped8(idx):
    return np.asarray(idx).reshape(8, -1, 16).transpose(0, 2, 1).reshape(128, -1).astype(np.uint16)


def unstriped8(offs):
    return offs.reshape(8, 16, -1).transpose(0, 2, 1).reshape(8, -1).astype(np.int64)


def pick8(x, idx, run):
    r = np.arange(len(x))
    return x[r[:, None], idx[r % (8 * run) // run]]


E2M1 = np.array([0.0, 0.5, 1.0, 1.5, 2.0, 3.0, 4.0, 6.0, -0.0, -0.5, -1.0, -1.5, -2.0, -3.0, -4.0, -6.0])


def pack_weight(w, fmt):
    k, n = w.shape
    w = f64(np.asarray(w, np.float32).astype(ml_dtypes.bfloat16)).reshape(k // 32, 32, n)
    amax = np.abs(w).max(1)
    if fmt == "e4m3":
        byte = np.frexp(amax)[1] - 1 + 127 - 7
    else:
        mant, ex = np.frexp(amax / 6.0)
        byte = np.where(mant > 0.5, ex, ex - 1) + 127
    byte = np.clip(np.where(amax > 0, byte, 1), 1, 254)
    scaled = (w * np.exp2(127.0 - byte)[:, None, :]).reshape(k, n).astype(np.float32)
    by_word = np.ascontiguousarray(scaled.reshape(k // 512, 128, 4, n).transpose(0, 1, 3, 2))
    if fmt == "e4m3":
        words = by_word.astype(ml_dtypes.float8_e4m3fn).view(np.uint8)
    else:
        c = by_word.astype(ml_dtypes.float4_e2m1fn).view(np.uint8) & 0xF
        words = (c[..., 0::2] | (c[..., 1::2] << 4)).reshape(k // 512, 128, 2 * n)
    return np.ascontiguousarray(words), np.ascontiguousarray(byte.astype(np.uint8).reshape(k // 512, 16, n))


def unpack_weight(words, scales, fmt):
    g, _, n = scales.shape
    words = np.ascontiguousarray(words).reshape(g, 128, n, -1)
    if fmt == "e4m3":
        vals = words.view(ml_dtypes.float8_e4m3fn).astype(np.float64)
    else:
        nib = np.empty((g, 128, n, 4), np.uint8)
        nib[..., 0::2] = words & 0xF
        nib[..., 1::2] = words >> 4
        vals = E2M1[nib]
    vals = vals * np.repeat(np.exp2(scales.astype(np.float64) - 127.0), 8, axis=1)[..., None]
    return vals.transpose(0, 1, 3, 2).reshape(g * 512, n)


K, L, T, J, N = 1024, 512, 1024, 512, 512


def setup_inputs():
    n = np.random.standard_normal
    idx = np.stack([np.random.permutation(T)[:J] for _ in range(8)])
    idx2 = np.stack([np.random.permutation(T)[:J] for _ in range(8)])
    fk = mx_kscale(K)
    fl = mx_kscale(L)
    xap = pack_weight(n((K, J)) / fk[:, None], "e4m3")
    wap = pack_weight(n((K, N)) * 1 / np.sqrt(K) * fk[:, None], "e2m1")
    wbp = pack_weight(n((L, N)) * 1 / np.sqrt(L) * fl[:, None], "e4m3")
    return {
        "xa_words": xap[0],
        "xa_scales": xap[1],
        "wa_words": wap[0],
        "wa_scales": wap[1],
        "xb": (n((L, J)) / fl[:, None]).astype(np.float32),
        "wb_words": wbp[0],
        "wb_scales": wbp[1],
        "res": (1.0 * n((N, T))).astype(np.float32),
        "offs": striped8(idx),
        "offs2": striped8(idx2),
    }


def reference(xa_words, xa_scales, wa_words, wa_scales, xb, wb_words, wb_scales, res, offs, offs2):
    idx = unstriped8(offs)
    idx2 = unstriped8(offs2)
    xau = unpack_weight(xa_words, xa_scales, "e4m3")
    wau = unpack_weight(wa_words, wa_scales, "e2m1")
    wbu = unpack_weight(wb_words, wb_scales, "e4m3")
    p = wau.T @ xau
    xbq = mxq(f64(xb), 0, "e4m3")
    q = wbu.T @ xbq
    pg = np.zeros((N, T))
    pg[np.arange(N)[:, None], idx[np.arange(N) % 512 // 64]] = p
    qg = np.zeros((N, T))
    qg[np.arange(N)[:, None], idx2[np.arange(N) % 512 // 64]] = q
    y = np.maximum(pg, qg) + 0.3 * f64(res)
    return y

@@ -1,0 +1,252 @@
+from contextlib import ExitStack
+
+import concourse.mybir as mybir
+from concourse.masks import make_identity
+
+K, L, T, J, N = 1024, 512, 1024, 512, 512
+FLOPS = 2 * (K + L) * N * J
+
+F32 = mybir.dt.float32
+BF16 = mybir.dt.bfloat16
+I32 = mybir.dt.int32
+U32 = mybir.dt.uint32
+U16 = mybir.dt.uint16
+U8 = mybir.dt.uint8
+FP8X4 = mybir.dt.float8_e4m3fn_x4
+FP4X4 = mybir.dt.float4_e2m1fn_x4
+ACT = mybir.ActivationFunctionType
+ALU = mybir.AluOpType
+
+P = 128
+TILES = N // P
+BANK = 512
+RES_WEIGHT = 0.3
+
+
+def tile_moe_heads_of_two_experts_kernel(
+    tc, xa_words, xa_scales, wa_words, wa_scales, xb, wb_words, wb_scales, res, offs, offs2, out
+):
+    nc = tc.nc
+    passes = K // 512
+    res_rows = res.rearrange("(p i) t -> p i t", i=TILES)
+    out_rows = out.rearrange("(p i) t -> p i t", i=TILES)
+
+    with ExitStack() as ctx:
+        keep = ctx.enter_context(tc.tile_pool(name="keep", bufs=1))
+        ring = ctx.enter_context(tc.tile_pool(name="ring", bufs=2))
+        shared = ctx.enter_context(tc.tile_pool(name="shared", bufs=1))
+        psum = ctx.enter_context(tc.psum_pool(name="psum", bufs=2))
+
+        def load_scale_rows(plane, scales):
+            rows = scales.bitcast(I32).rearrange("z (g r) c -> r g z c", r=4)
+            for r in range(4):
+                nc.sync.dma_start(plane[:].bitcast(I32)[r:P:32], rows[r])
+
+        wa_scale_raw = keep.tile([P, passes, N], U8, align_bytes=64)
+        xa_scale = keep.tile([P, passes, J], U8, align_bytes=64)
+        wb_scale_raw = shared.tile([P, 1, N], U8, offset=4 * 4 * J)
+        for plane in (wa_scale_raw, xa_scale, wb_scale_raw):
+            nc.gpsimd.memset(plane[:].bitcast(I32), 0)
+
+        wa_raw = keep.tile([P, passes, 2 * N], U8, align_bytes=64)
+        nc.sync.dma_start(wa_raw[:].bitcast(I32), wa_words.bitcast(I32).rearrange("z p c -> p z c"))
+        xa_code = keep.tile([P, passes, J], U32, align_bytes=64)
+        xa_by_partition = xa_words.rearrange("z p c r -> p z (c r)").bitcast(I32)
+        nc.sync.dma_start(xa_code[:].bitcast(I32)[:, :, 0 : J // 2], xa_by_partition[:, :, 0 : J // 2])
+        load_scale_rows(wa_scale_raw, wa_scales)
+        load_scale_rows(xa_scale, xa_scales)
+        list_a = keep.tile([P, J // 16], U16)
+        nc.sync.dma_start(list_a[:], offs)
+        nc.sync.dma_start(xa_code[:].bitcast(I32)[:, :, J // 2 : J], xa_by_partition[:, :, J // 2 : J])
+
+        xb_rows = xb.rearrange("(p r) j -> p r j", r=4)
+        xb_raw = shared.tile([P, 4, J], F32, offset=0)
+        slot_halves = [slice(0, J // 2), slice(J // 2, J)]
+        for cols in slot_halves:
+            nc.sync.dma_start(xb_raw[:, :, cols], xb_rows[:, :, cols])
+        wb_raw = keep.tile([P, N], U32, align_bytes=64)
+        nc.sync.dma_start(
+            wb_raw[:].bitcast(I32), wb_words[0].rearrange("p c r -> p (c r)").bitcast(I32)
+        )
+        load_scale_rows(wb_scale_raw, wb_scales)
+        list_b = keep.tile([P, J // 16], U16)
+        nc.sync.dma_start(list_b[:], offs2)
+        res_sb = []
+        for i in range(TILES):
+            rows = keep.tile([P, T], F32, name="res%d" % i)
+            nc.sync.dma_start(rows[:], res_rows[:, i, :])
+            res_sb.append(rows)
+
+        identity = keep.tile([P, P], F32)
+        make_identity(nc, identity[:])
+
+        wa_code, wa_scale = [], []
+        for lo, hi in ((0, 1), (1, TILES)):
+            code = keep.tile([P, passes, hi - lo, 2 * P], U8, name="wa_code%d" % lo, align_bytes=64)
+            scale = keep.tile([P, passes, hi - lo, P], U8, name="wa_scale%d" % lo, align_bytes=64)
+            nc.vector.tensor_copy(
+                code[:].bitcast(U16),
+                wa_raw[:].bitcast(U16).rearrange("p z (m i) -> p z i m", i=TILES)[:, :, lo:hi, :],
+            )
+            nc.vector.tensor_copy(
+                scale[:],
+                wa_scale_raw[:].rearrange("p z (m i) -> p z i m", i=TILES)[:, :, lo:hi, :],
+            )
+            for i in range(hi - lo):
+                wa_code.append([code[:, z, i, :].bitcast(FP4X4) for z in range(passes)])
+                wa_scale.append([scale[:, z, i, :] for z in range(passes)])
+
+        windows = []
+        for w in range(4):
+            window = keep.tile([P, T], F32, name="window%d" % w)
+            nc.vector.memset(window[:].bitcast(I32), 0)
+            windows.append(window)
+        window_a = [windows[0], windows[1], windows[0], windows[1]]
+        window_b = [windows[2], windows[3], windows[2], windows[3]]
+
+        def product_a(i):
+            acc = psum.tile([P, J], F32, tag="product", bufs=6, name="acc_a%d" % i)
+            for z in range(passes):
+                nc.tensor.matmul_mx(
+                    acc[:],
+                    lhsT=wa_code[i][z],
+                    lhsT_scale=wa_scale[i][z],
+                    rhs=xa_code[:, z, :].bitcast(FP8X4),
+                    rhs_scale=xa_scale[:, z, :],
+                    start=(z == 0),
+                    stop=(z == passes - 1),
+                )
+            return acc
+
+        def place(window, offsets, acc, staged, factor):
+            nc.scalar.activation(staged, acc[:], ACT.Copy, scale=factor)
+            nc.vector.tensor_copy(window[:].indirect(offsets), staged)
+
+        def fresh(name):
+            staged = keep.tile([P, J], F32, name=name)
+            return staged[:]
+
+        last = TILES - 1
+        factor_a = [1.0 / RES_WEIGHT] * last + [1.0]
+        factor_b = [-1.0 / RES_WEIGHT] * last + [1.0]
+
+        for lo, hi in ((0, 128), (128, 256), (256, 512)):
+            acc = psum.tile([P, hi - lo], F32, tag="product", bufs=6, name="acc_first%d" % lo)
+            for c in range(lo, hi, P):
+                for z in range(passes):
+                    nc.tensor.matmul_mx(
+                        acc[:, c - lo : c - lo + P],
+                        lhsT=wa_code[0][z],
+                        lhsT_scale=wa_scale[0][z],
+                        rhs=xa_code[:, z, c : c + P].bitcast(FP8X4),
+                        rhs_scale=xa_scale[:, z, c : c + P],
+                        start=(z == 0),
+                        stop=(z == passes - 1),
+                    )
+            piece = keep.tile([P, hi - lo], F32, name="staged_first%d" % lo)
+            place(window_a[0], list_a[:, lo // 16 : hi // 16], acc, piece[:], factor_a[0])
+
+        wb_code = keep.tile([P, TILES, P], U32, align_bytes=64)
+        wb_scale = keep.tile([P, TILES, P], U8, align_bytes=64)
+        nc.vector.tensor_copy(wb_code[:], wb_raw[:].rearrange("p (m i) -> p i m", i=TILES))
+        nc.vector.tensor_copy(wb_scale[:], wb_scale_raw[:, 0, :].rearrange("p (m i) -> p i m", i=TILES))
+
+        xb_grouped = keep.tile([P, J, 4], BF16, align_bytes=64)
+        for cols in slot_halves:
+            nc.scalar.copy(
+                xb_grouped[:, cols, :].rearrange("p (c u) r -> p c r u", u=4),
+                xb_raw[:, :, cols].rearrange("p r (c u) -> p c r u", u=4),
+            )
+        xb_code = keep.tile([P, J], U32, align_bytes=64)
+        xb_scale = keep.tile([P, J], U8, align_bytes=64)
+        nc.vector.quantize_mx(
+            xb_code[:].bitcast(FP8X4), xb_scale[:], xb_grouped[:].rearrange("p j r -> p (j r)")
+        )
+
+        def product_b(i):
+            if i < 2:
+                acc = psum.tile([P, J], F32, tag="turning", name="acc_b%d" % i)
+            else:
+                acc = psum.tile([P, J], F32, tag="product", bufs=6, name="acc_b%d" % i)
+            nc.tensor.matmul_mx(
+                acc[:],
+                lhsT=wb_code[:, i, :].bitcast(FP8X4),
+                lhsT_scale=wb_scale[:, i, :],
+                rhs=xb_code[:].bitcast(FP8X4),
+                rhs_scale=xb_scale[:],
+                start=True,
+                stop=True,
+            )
+            return acc
+
+        def turned_sum(tag, first, second):
+            bank = psum.tile([P, BANK], F32, tag="turning", name=tag)
+            for b in range(BANK // P):
+                cols = slice(b * P, (b + 1) * P)
+                nc.tensor.matmul(bank[:, cols], first[:, cols], identity[:], start=True, stop=False, is_transpose=True)
+                nc.tensor.matmul(bank[:, cols], second[:, cols], identity[:], start=False, stop=True, is_transpose=True)
+            return bank
+
+        halves = [slice(h * BANK, (h + 1) * BANK) for h in range(T // BANK)]
+
+        def base(i):
+            turned = []
+            for cols in halves:
+                bank = turned_sum("base", window_a[i][:, cols], res_sb[i][:, cols])
+                moved = ring.tile([P, BANK], F32, tag="base_t", name="base_t", bufs=4)
+                nc.scalar.copy(moved[:], bank[:])
+                turned.append(moved)
+            return turned
+
+        def combine(i, base_t):
+            excess_t = []
+            for cols in halves:
+                bank = turned_sum("gap", window_a[i][:, cols], window_b[i][:, cols])
+                excess = ring.tile([P, BANK], F32, tag="excess_t", name="excess_t")
+                nc.scalar.activation(excess[:], bank[:], ACT.Relu, scale=-1.0)
+                excess_t.append(excess)
+            for h, cols in enumerate(halves):
+                bank = turned_sum("total", base_t[h][:], excess_t[h][:])
+                result = ring.tile([P, BANK], F32, tag="result", name="result", bufs=4)
+                nc.scalar.activation(result[:], bank[:], ACT.Copy, scale=RES_WEIGHT)
+                nc.sync.dma_start(out_rows[:, i, cols], result[:])
+
+        def stage(acc, staged, factor):
+            nc.scalar.activation(staged, acc[:], ACT.Copy, scale=factor)
+            return staged
+
+        def scatter(window, offsets, staged):
+            nc.vector.tensor_copy(window[:].indirect(offsets[:]), staged)
+
+        acc_a = [product_a(i) for i in range(1, TILES)]
+        values_a = [None]
+        for i, offset in ((1, 3 * 4 * J + N), (2, 0), (3, 4 * J)):
+            reused = shared.tile([P, J], F32, name="staged_a%d" % i, offset=offset)
+            values_a.append(stage(acc_a[i - 1], reused[:], factor_a[i]))
+        values_b = [stage(product_b(i), fresh("staged_b%d" % i), factor_b[i]) for i in range(TILES)]
+        scatter(window_a[1], list_a, values_a[1])
+        scatter(window_b[0], list_b, values_b[0])
+        scatter(window_b[1], list_b, values_b[1])
+        base0 = base(0)
+        base1 = base(1)
+        combine(0, base0)
+        scatter(window_a[2], list_a, values_a[2])
+        scatter(window_b[2], list_b, values_b[2])
+        combine(1, base1)
+        scatter(window_a[3], list_a, values_a[3])
+        scatter(window_b[3], list_b, values_b[3])
+        combine(2, base(2))
+
+        larger = keep.tile([P, T], F32)
+        final = keep.tile([P, T], F32)
+        quarters = [slice(c, c + T // 4) for c in range(0, T, T // 4)]
+        for step in range(len(quarters) + 1):
+            if step < len(quarters):
+                cols = quarters[step]
+                nc.vector.tensor_tensor(larger[:, cols], window_a[last][:, cols], window_b[last][:, cols], ALU.max)
+            if step > 0:
+                cols = quarters[step - 1]
+                nc.vector.scalar_tensor_tensor(
+                    final[:, cols], res_sb[last][:, cols], RES_WEIGHT, larger[:, cols], ALU.mult, ALU.add
+                )
+                nc.sync.dma_start(out_rows[:, last, cols], final[:, cols])

@@ -48,12 +48,12 @@ def tile_moe_heads_of_two_experts_kernel(
         for plane in (wa_scale_raw, xa_scale, wb_scale_raw):
             nc.gpsimd.memset(plane[:].bitcast(I32), 0)
 
+        load_scale_rows(wa_scale_raw, wa_scales)
         wa_raw = keep.tile([P, passes, 2 * N], U8, align_bytes=64)
         nc.sync.dma_start(wa_raw[:].bitcast(I32), wa_words.bitcast(I32).rearrange("z p c -> p z c"))
         xa_code = keep.tile([P, passes, J], U32, align_bytes=64)
         xa_by_partition = xa_words.rearrange("z p c r -> p z (c r)").bitcast(I32)
         nc.sync.dma_start(xa_code[:].bitcast(I32)[:, :, 0 : J // 2], xa_by_partition[:, :, 0 : J // 2])
-        load_scale_rows(wa_scale_raw, wa_scales)
         load_scale_rows(xa_scale, xa_scales)
         list_a = keep.tile([P, J // 16], U16)
         nc.sync.dma_start(list_a[:], offs)
@@ -64,7 +64,7 @@ def tile_moe_heads_of_two_experts_kernel(
         slot_halves = [slice(0, J // 2), slice(J // 2, J)]
         for cols in slot_halves:
             nc.sync.dma_start(xb_raw[:, :, cols], xb_rows[:, :, cols])
-        wb_raw = keep.tile([P, N], U32, align_bytes=64)
+        wb_raw = shared.tile([P, N], U32, align_bytes=64, offset=10688)
         nc.sync.dma_start(
             wb_raw[:].bitcast(I32), wb_words[0].rearrange("p c r -> p (c r)").bitcast(I32)
         )
@@ -99,7 +99,8 @@ def tile_moe_heads_of_two_experts_kernel(
         windows = []
         for w in range(4):
             window = keep.tile([P, T], F32, name="window%d" % w)
-            nc.vector.memset(window[:].bitcast(I32), 0)
+            for cols in (slice(0, 511), slice(511, T)) if w == 0 else (slice(0, T),):
+                nc.vector.memset(window[:].bitcast(I32)[:, cols], 0)
             windows.append(window)
         window_a = [windows[0], windows[1], windows[0], windows[1]]
         window_b = [windows[2], windows[3], windows[2], windows[3]]
@@ -146,10 +147,13 @@ def tile_moe_heads_of_two_experts_kernel(
             piece = keep.tile([P, hi - lo], F32, name="staged_first%d" % lo)
             place(window_a[0], list_a[:, lo // 16 : hi // 16], acc, piece[:], factor_a[0])
 
-        wb_code = keep.tile([P, TILES, P], U32, align_bytes=64)
+        wb_code = shared.tile([P, TILES, P], U32, align_bytes=64, offset=8640)
         wb_scale = keep.tile([P, TILES, P], U8, align_bytes=64)
-        nc.vector.tensor_copy(wb_code[:], wb_raw[:].rearrange("p (m i) -> p i m", i=TILES))
         nc.vector.tensor_copy(wb_scale[:], wb_scale_raw[:, 0, :].rearrange("p (m i) -> p i m", i=TILES))
+        nc.vector.tensor_copy(
+            wb_code[:].rearrange("p i (c u) -> p c i u", u=4),
+            wb_raw[:].rearrange("p (c u i) -> p c i u", u=4, i=TILES),
+        )
 
         xb_grouped = keep.tile([P, J, 4], BF16, align_bytes=64)
         for cols in slot_halves:
@@ -157,7 +161,7 @@ def tile_moe_heads_of_two_experts_kernel(
                 xb_grouped[:, cols, :].rearrange("p (c u) r -> p c r u", u=4),
                 xb_raw[:, :, cols].rearrange("p r (c u) -> p c r u", u=4),
             )
-        xb_code = keep.tile([P, J], U32, align_bytes=64)
+        xb_code = shared.tile([P, J], U32, align_bytes=64, offset=10688)
         xb_scale = keep.tile([P, J], U8, align_bytes=64)
         nc.vector.quantize_mx(
             xb_code[:].bitcast(FP8X4), xb_scale[:], xb_grouped[:].rearrange("p j r -> p (j r)")
@@ -220,7 +224,7 @@ def tile_moe_heads_of_two_experts_kernel(
 
         acc_a = [product_a(i) for i in range(1, TILES)]
         values_a = [None]
-        for i, offset in ((1, 3 * 4 * J + N), (2, 0), (3, 4 * J)):
+        for i, offset in ((1, 6208), (2, 0), (3, 4 * J)):
             reused = shared.tile([P, J], F32, name="staged_a%d" % i, offset=offset)
             values_a.append(stage(acc_a[i - 1], reused[:], factor_a[i]))
         values_b = [stage(product_b(i), fresh("staged_b%d" % i), factor_b[i]) for i in range(TILES)]
@@ -239,7 +243,7 @@ def tile_moe_heads_of_two_experts_kernel(
 
         larger = keep.tile([P, T], F32)
         final = keep.tile([P, T], F32)
-        quarters = [slice(c, c + T // 4) for c in range(0, T, T // 4)]
+        quarters = [slice(0, 320), slice(320, 640), slice(640, 896), slice(896, T)]
         for step in range(len(quarters) + 1):
             if step < len(quarters):
                 cols = quarters[step]

from contextlib import ExitStack

import concourse.mybir as mybir
from concourse.masks import make_identity

K, L, T, J, N = 1024, 512, 1024, 512, 512
FLOPS = 2 * (K + L) * N * J

F32 = mybir.dt.float32
BF16 = mybir.dt.bfloat16
I32 = mybir.dt.int32
U32 = mybir.dt.uint32
U16 = mybir.dt.uint16
U8 = mybir.dt.uint8
FP8X4 = mybir.dt.float8_e4m3fn_x4
FP4X4 = mybir.dt.float4_e2m1fn_x4
ACT = mybir.ActivationFunctionType
ALU = mybir.AluOpType

P = 128
TILES = N // P
BANK = 512
RES_WEIGHT = 0.3


def tile_moe_heads_of_two_experts_kernel(
    tc, xa_words, xa_scales, wa_words, wa_scales, xb, wb_words, wb_scales, res, offs, offs2, out
):
    nc = tc.nc
    passes = K // 512
    res_rows = res.rearrange("(p i) t -> p i t", i=TILES)
    out_rows = out.rearrange("(p i) t -> p i t", i=TILES)

    with ExitStack() as ctx:
        keep = ctx.enter_context(tc.tile_pool(name="keep", bufs=1))
        ring = ctx.enter_context(tc.tile_pool(name="ring", bufs=2))
        shared = ctx.enter_context(tc.tile_pool(name="shared", bufs=1))
        psum = ctx.enter_context(tc.psum_pool(name="psum", bufs=2))

        def load_scale_rows(plane, scales):
            rows = scales.bitcast(I32).rearrange("z (g r) c -> r g z c", r=4)
            for r in range(4):
                nc.sync.dma_start(plane[:].bitcast(I32)[r:P:32], rows[r])

        wa_scale_raw = keep.tile([P, passes, N], U8, align_bytes=64)
        xa_scale = keep.tile([P, passes, J], U8, align_bytes=64)
        wb_scale_raw = shared.tile([P, 1, N], U8, offset=4 * 4 * J)
        for plane in (wa_scale_raw, xa_scale, wb_scale_raw):
            nc.gpsimd.memset(plane[:].bitcast(I32), 0)

        load_scale_rows(wa_scale_raw, wa_scales)
        wa_raw = keep.tile([P, passes, 2 * N], U8, align_bytes=64)
        nc.sync.dma_start(wa_raw[:].bitcast(I32), wa_words.bitcast(I32).rearrange("z p c -> p z c"))
        xa_code = keep.tile([P, passes, J], U32, align_bytes=64)
        xa_by_partition = xa_words.rearrange("z p c r -> p z (c r)").bitcast(I32)
        nc.sync.dma_start(xa_code[:].bitcast(I32)[:, :, 0 : J // 2], xa_by_partition[:, :, 0 : J // 2])
        load_scale_rows(xa_scale, xa_scales)
        list_a = keep.tile([P, J // 16], U16)
        nc.sync.dma_start(list_a[:], offs)
        nc.sync.dma_start(xa_code[:].bitcast(I32)[:, :, J // 2 : J], xa_by_partition[:, :, J // 2 : J])

        xb_rows = xb.rearrange("(p r) j -> p r j", r=4)
        xb_raw = shared.tile([P, 4, J], F32, offset=0)
        slot_halves = [slice(0, J // 2), slice(J // 2, J)]
        for cols in slot_halves:
            nc.sync.dma_start(xb_raw[:, :, cols], xb_rows[:, :, cols])
        wb_raw = shared.tile([P, N], U32, align_bytes=64, offset=10688)
        nc.sync.dma_start(
            wb_raw[:].bitcast(I32), wb_words[0].rearrange("p c r -> p (c r)").bitcast(I32)
        )
        load_scale_rows(wb_scale_raw, wb_scales)
        list_b = keep.tile([P, J // 16], U16)
        nc.sync.dma_start(list_b[:], offs2)
        res_sb = []
        for i in range(TILES):
            rows = keep.tile([P, T], F32, name="res%d" % i)
            nc.sync.dma_start(rows[:], res_rows[:, i, :])
            res_sb.append(rows)

        identity = keep.tile([P, P], F32)
        make_identity(nc, identity[:])

        wa_code, wa_scale = [], []
        for lo, hi in ((0, 1), (1, TILES)):
            code = keep.tile([P, passes, hi - lo, 2 * P], U8, name="wa_code%d" % lo, align_bytes=64)
            scale = keep.tile([P, passes, hi - lo, P], U8, name="wa_scale%d" % lo, align_bytes=64)
            nc.vector.tensor_copy(
                code[:].bitcast(U16),
                wa_raw[:].bitcast(U16).rearrange("p z (m i) -> p z i m", i=TILES)[:, :, lo:hi, :],
            )
            nc.vector.tensor_copy(
                scale[:],
                wa_scale_raw[:].rearrange("p z (m i) -> p z i m", i=TILES)[:, :, lo:hi, :],
            )
            for i in range(hi - lo):
                wa_code.append([code[:, z, i, :].bitcast(FP4X4) for z in range(passes)])
                wa_scale.append([scale[:, z, i, :] for z in range(passes)])

        windows = []
        for w in range(4):
            window = keep.tile([P, T], F32, name="window%d" % w)
            for cols in (slice(0, 511), slice(511, T)) if w == 0 else (slice(0, T),):
                nc.vector.memset(window[:].bitcast(I32)[:, cols], 0)
            windows.append(window)
        window_a = [windows[0], windows[1], windows[0], windows[1]]
        window_b = [windows[2], windows[3], windows[2], windows[3]]

        def product_a(i):
            acc = psum.tile([P, J], F32, tag="product", bufs=6, name="acc_a%d" % i)
            for z in range(passes):
                nc.tensor.matmul_mx(
                    acc[:],
                    lhsT=wa_code[i][z],
                    lhsT_scale=wa_scale[i][z],
                    rhs=xa_code[:, z, :].bitcast(FP8X4),
                    rhs_scale=xa_scale[:, z, :],
                    start=(z == 0),
                    stop=(z == passes - 1),
                )
            return acc

        def place(window, offsets, acc, staged, factor):
            nc.scalar.activation(staged, acc[:], ACT.Copy, scale=factor)
            nc.vector.tensor_copy(window[:].indirect(offsets), staged)

        def fresh(name):
            staged = keep.tile([P, J], F32, name=name)
            return staged[:]

        last = TILES - 1
        factor_a = [1.0 / RES_WEIGHT] * last + [1.0]
        factor_b = [-1.0 / RES_WEIGHT] * last + [1.0]

        for lo, hi in ((0, 128), (128, 256), (256, 512)):
            acc = psum.tile([P, hi - lo], F32, tag="product", bufs=6, name="acc_first%d" % lo)
            for c in range(lo, hi, P):
                for z in range(passes):
                    nc.tensor.matmul_mx(
                        acc[:, c - lo : c - lo + P],
                        lhsT=wa_code[0][z],
                        lhsT_scale=wa_scale[0][z],
                        rhs=xa_code[:, z, c : c + P].bitcast(FP8X4),
                        rhs_scale=xa_scale[:, z, c : c + P],
                        start=(z == 0),
                        stop=(z == passes - 1),
                    )
            piece = keep.tile([P, hi - lo], F32, name="staged_first%d" % lo)
            place(window_a[0], list_a[:, lo // 16 : hi // 16], acc, piece[:], factor_a[0])

        wb_code = shared.tile([P, TILES, P], U32, align_bytes=64, offset=8640)
        wb_scale = keep.tile([P, TILES, P], U8, align_bytes=64)
        nc.vector.tensor_copy(wb_scale[:], wb_scale_raw[:, 0, :].rearrange("p (m i) -> p i m", i=TILES))
        nc.vector.tensor_copy(
            wb_code[:].rearrange("p i (c u) -> p c i u", u=4),
            wb_raw[:].rearrange("p (c u i) -> p c i u", u=4, i=TILES),
        )

        xb_grouped = keep.tile([P, J, 4], BF16, align_bytes=64)
        for cols in slot_halves:
            nc.scalar.copy(
                xb_grouped[:, cols, :].rearrange("p (c u) r -> p c r u", u=4),
                xb_raw[:, :, cols].rearrange("p r (c u) -> p c r u", u=4),
            )
        xb_code = shared.tile([P, J], U32, align_bytes=64, offset=10688)
        xb_scale = keep.tile([P, J], U8, align_bytes=64)
        nc.vector.quantize_mx(
            xb_code[:].bitcast(FP8X4), xb_scale[:], xb_grouped[:].rearrange("p j r -> p (j r)")
        )

        def product_b(i):
            if i < 2:
                acc = psum.tile([P, J], F32, tag="turning", name="acc_b%d" % i)
            else:
                acc = psum.tile([P, J], F32, tag="product", bufs=6, name="acc_b%d" % i)
            nc.tensor.matmul_mx(
                acc[:],
                lhsT=wb_code[:, i, :].bitcast(FP8X4),
                lhsT_scale=wb_scale[:, i, :],
                rhs=xb_code[:].bitcast(FP8X4),
                rhs_scale=xb_scale[:],
                start=True,
                stop=True,
            )
            return acc

        def turned_sum(tag, first, second):
            bank = psum.tile([P, BANK], F32, tag="turning", name=tag)
            for b in range(BANK // P):
                cols = slice(b * P, (b + 1) * P)
                nc.tensor.matmul(bank[:, cols], first[:, cols], identity[:], start=True, stop=False, is_transpose=True)
                nc.tensor.matmul(bank[:, cols], second[:, cols], identity[:], start=False, stop=True, is_transpose=True)
            return bank

        halves = [slice(h * BANK, (h + 1) * BANK) for h in range(T // BANK)]

        def base(i):
            turned = []
            for cols in halves:
                bank = turned_sum("base", window_a[i][:, cols], res_sb[i][:, cols])
                moved = ring.tile([P, BANK], F32, tag="base_t", name="base_t", bufs=4)
                nc.scalar.copy(moved[:], bank[:])
                turned.append(moved)
            return turned

        def combine(i, base_t):
            excess_t = []
            for cols in halves:
                bank = turned_sum("gap", window_a[i][:, cols], window_b[i][:, cols])
                excess = ring.tile([P, BANK], F32, tag="excess_t", name="excess_t")
                nc.scalar.activation(excess[:], bank[:], ACT.Relu, scale=-1.0)
                excess_t.append(excess)
            for h, cols in enumerate(halves):
                bank = turned_sum("total", base_t[h][:], excess_t[h][:])
                result = ring.tile([P, BANK], F32, tag="result", name="result", bufs=4)
                nc.scalar.activation(result[:], bank[:], ACT.Copy, scale=RES_WEIGHT)
                nc.sync.dma_start(out_rows[:, i, cols], result[:])

        def stage(acc, staged, factor):
            nc.scalar.activation(staged, acc[:], ACT.Copy, scale=factor)
            return staged

        def scatter(window, offsets, staged):
            nc.vector.tensor_copy(window[:].indirect(offsets[:]), staged)

        acc_a = [product_a(i) for i in range(1, TILES)]
        values_a = [None]
        for i, offset in ((1, 6208), (2, 0), (3, 4 * J)):
            reused = shared.tile([P, J], F32, name="staged_a%d" % i, offset=offset)
            values_a.append(stage(acc_a[i - 1], reused[:], factor_a[i]))
        values_b = [stage(product_b(i), fresh("staged_b%d" % i), factor_b[i]) for i in range(TILES)]
        scatter(window_a[1], list_a, values_a[1])
        scatter(window_b[0], list_b, values_b[0])
        scatter(window_b[1], list_b, values_b[1])
        base0 = base(0)
        base1 = base(1)
        combine(0, base0)
        scatter(window_a[2], list_a, values_a[2])
        scatter(window_b[2], list_b, values_b[2])
        combine(1, base1)
        scatter(window_a[3], list_a, values_a[3])
        scatter(window_b[3], list_b, values_b[3])
        combine(2, base(2))

        larger = keep.tile([P, T], F32)
        final = keep.tile([P, T], F32)
        quarters = [slice(0, 320), slice(320, 640), slice(640, 896), slice(896, T)]
        for step in range(len(quarters) + 1):
            if step < len(quarters):
                cols = quarters[step]
                nc.vector.tensor_tensor(larger[:, cols], window_a[last][:, cols], window_b[last][:, cols], ALU.max)
            if step > 0:
                cols = quarters[step - 1]
                nc.vector.scalar_tensor_tensor(
                    final[:, cols], res_sb[last][:, cols], RES_WEIGHT, larger[:, cols], ALU.mult, ALU.add
                )
                nc.sync.dma_start(out_rows[:, last, cols], final[:, cols])
